import numpy as np
import ml_dtypes


def mxq(x, axis, fmt="e4m3"):
    dtype, down = {"e4m3": (ml_dtypes.float8_e4m3fn, 7), "e5m2": (ml_dtypes.float8_e5m2, 14)}[fmt]
    v = np.moveaxis(np.asarray(x, np.float32).astype(ml_dtypes.bfloat16).astype(np.float64), axis, -1)
    blocks = v.reshape(v.shape[:-1] + (-1, 32))
    amax = np.abs(blocks).max(-1, keepdims=True)
    byte = np.maximum(np.where(amax > 0, np.frexp(amax)[1] - 1 + 127, 0) - down, 1)
    scale = np.exp2(byte - 127.0)
    codes = (blocks / scale).astype(np.float32).astype(dtype).astype(np.float64)
    return np.moveaxis((codes * scale).reshape(v.shape), -1, axis)


WIDE = False


def mx_kscale(k):
    if not WIDE:
        return np.ones(k)
    levels = np.array([30, -30])
    if k % 512:
        return np.exp2(np.random.permutation(np.resize(levels, k // 32))).repeat(32)
    a = np.empty((k // 512, 16))
    for p in range(k // 512):
        a[p, :8] = np.random.permutation(np.resize(levels, 8))
        for g in range(8):
            far = levels[np.abs(levels - a[p, g]) >= 10]
            a[p, g + 8] = far[np.random.randint(len(far))]
    return np.exp2(a.ravel()).repeat(32)


def f64(x):
    return np.asarray(x).astype(np.float64)


def striped(idx):
    return np.tile(np.asarray(idx).reshape(-1, 16).T, (8, 1)).astype(np.uint16)


def unstriped(offs):
    return offs[:16].T.reshape(-1).astype(np.int64)


E2M1 = np.array([0.0, 0.5, 1.0, 1.5, 2.0, 3.0, 4.0, 6.0, -0.0, -0.5, -1.0, -1.5, -2.0, -3.0, -4.0, -6.0])


def pack_weight(w, fmt):
    k, n = w.shape
    w = f64(np.asarray(w, np.float32).astype(ml_dtypes.bfloat16)).reshape(k // 32, 32, n)
    amax = np.abs(w).max(1)
    if fmt in ("e4m3", "e5m2"):
        byte = np.frexp(amax)[1] - 1 + 127 - (7 if fmt == "e4m3" else 14)
    else:
        mant, ex = np.frexp(amax / 6.0)
        byte = np.where(mant > 0.5, ex, ex - 1) + 127
    byte = np.clip(np.where(amax > 0, byte, 1), 1, 254)
    scaled = (w * np.exp2(127.0 - byte)[:, None, :]).reshape(k, n).astype(np.float32)
    by_word = np.ascontiguousarray(scaled.reshape(k // 512, 128, 4, n).transpose(0, 1, 3, 2))
    if fmt in ("e4m3", "e5m2"):
        words = by_word.astype(ml_dtypes.float8_e4m3fn if fmt == "e4m3" else ml_dtypes.float8_e5m2).view(np.uint8)
    else:
        c = by_word.astype(ml_dtypes.float4_e2m1fn).view(np.uint8) & 0xF
        words = (c[..., 0::2] | (c[..., 1::2] << 4)).reshape(k // 512, 128, 2 * n)
    return np.ascontiguousarray(words), np.ascontiguousarray(byte.astype(np.uint8).reshape(k // 512, 16, n))


def unpack_weight(words, scales, fmt):
    g, _, n = scales.shape
    words = np.ascontiguousarray(words).reshape(g, 128, n, -1)
    if fmt in ("e4m3", "e5m2"):
        vals = words.view(ml_dtypes.float8_e4m3fn if fmt == "e4m3" else ml_dtypes.float8_e5m2).astype(np.float64)
    else:
        nib = np.empty((g, 128, n, 4), np.uint8)
        nib[..., 0::2] = words & 0xF
        nib[..., 1::2] = words >> 4
        vals = E2M1[nib]
    vals = vals * np.repeat(np.exp2(scales.astype(np.float64) - 127.0), 8, axis=1)[..., None]
    return vals.transpose(0, 1, 3, 2).reshape(g * 512, n)


def sgn(shape):
    return np.random.uniform(0.5, 2.0, shape) * np.where(np.random.standard_normal(shape) < 0, -1.0, 1.0)


K, F, T, Z, J, R, O, N = 512, 512, 1024, 1024, 256, 512, 128, 256


def setup_inputs():
    n = np.random.standard_normal
    idx = np.random.permutation(T)[:J]
    idx2 = np.random.permutation(Z)[:J]
    idx3 = np.random.permutation(J)[:O]
    idx4 = np.random.permutation(J)[:O]
    idx5 = np.random.permutation(J)[:O]
    idx6 = np.random.permutation(T)[:O]
    fk = mx_kscale(K)
    fr = mx_kscale(R)
    ff = mx_kscale(F)
    xtp = pack_weight(n((K, T)) / fk[:, None], "e4m3")
    wp = pack_weight(n((K, R)) * 1 / np.sqrt(K) * fk[:, None] * fr, "e2m1")
    xop = pack_weight(n((F, Z)) / ff[:, None], "e2m1")
    w0p = pack_weight(n((F, R)) * 1 / np.sqrt(F) * ff[:, None] * fr, "e5m2")
    wbp = pack_weight(n((R, N)) * 1 / np.sqrt(R) / fr[:, None], "e5m2")
    wsp = pack_weight(n((K, N)) * 1 / np.sqrt(K) * fk[:, None], "e5m2")
    return {
        "xt_words": xtp[0],
        "xt_scales": xtp[1],
        "w_words": wp[0],
        "w_scales": wp[1],
        "xo_words": xop[0],
        "xo_scales": xop[1],
        "w0_words": w0p[0],
        "w0_scales": w0p[1],
        "sa": (sgn((R, 1))).astype(np.float32),
        "sb": (sgn((R, 1))).astype(np.float32),
        "sd": (sgn((R, 1))).astype(np.float32),
        "wb_words": wbp[0],
        "wb_scales": wbp[1],
        "ws_words": wsp[0],
        "ws_scales": wsp[1],
        "offs": striped(idx),
        "offs2": striped(idx2),
        "offs3": striped(idx3),
        "offs4": striped(idx4),
        "offs5": striped(idx5),
        "offs6": striped(idx6),
    }


def reference(xt_words, xt_scales, w_words, w_scales, xo_words, xo_scales, w0_words, w0_scales, sa, sb, sd, wb_words, wb_scales, ws_words, ws_scales, offs, offs2, offs3, offs4, offs5, offs6):
    idx = unstriped(offs)
    idx2 = unstriped(offs2)
    idx3 = unstriped(offs3)
    idx4 = unstriped(offs4)
    idx5 = unstriped(offs5)
    idx6 = unstriped(offs6)
    xtu = unpack_weight(xt_words, xt_scales, "e4m3")
    wu = unpack_weight(w_words, w_scales, "e2m1")
    xou = unpack_weight(xo_words, xo_scales, "e2m1")
    w0u = unpack_weight(w0_words, w0_scales, "e5m2")
    wbu = unpack_weight(wb_words, wb_scales, "e5m2")
    wsu = unpack_weight(ws_words, ws_scales, "e5m2")
    xtidxg = xtu[:, idx]
    xoidx2g = xou[:, idx2]
    a = wu.T @ xtidxg + w0u.T @ xoidx2g
    hid = np.maximum(a[:, idx3] * f64(sa) + a[:, idx4] * f64(sb) + a[:, idx5] * f64(sd), 0.0)
    hidq = mxq(hid, 0, "e4m3")
    xtidx6g = xtu[:, idx6]
    y = wbu.T @ hidq + wsu.T @ xtidx6g
    return y

@@ -1,0 +1,198 @@
+from contextlib import ExitStack
+
+import concourse.mybir as mybir
+
+K, F, T, Z, J, R, O, N = 512, 512, 1024, 1024, 256, 512, 128, 256
+FLOPS = 2 * (K * R * J + F * R * J + R * N * O + K * N * O)
+
+F32 = mybir.dt.float32
+BF16 = mybir.dt.bfloat16
+I32 = mybir.dt.int32
+U32 = mybir.dt.uint32
+U16 = mybir.dt.uint16
+U8 = mybir.dt.uint8
+E4M3 = mybir.dt.float8_e4m3fn_x4
+E5M2 = mybir.dt.float8_e5m2_x4
+E2M1 = mybir.dt.float4_e2m1fn_x4
+ALU = mybir.AluOpType
+ACT = mybir.ActivationFunctionType
+
+P = 128
+PACK = 4
+QUADS = 4
+QUAD = 32
+
+
+def tile_list_tripleblend_bank_further_plain_kernel(
+    tc, xt_words, xt_scales, w_words, w_scales, xo_words, xo_scales, w0_words, w0_scales, sa, sb, sd,
+    wb_words, wb_scales, ws_words, ws_scales, offs, offs2, offs3, offs4, offs5, offs6, out,
+):
+    nc = tc.nc
+    with ExitStack() as ctx:
+        keep = ctx.enter_context(tc.tile_pool(name="keep", bufs=1))
+        psum = ctx.enter_context(tc.psum_pool(name="psum", bufs=1))
+
+        def sb_tile(name, shape, dtype):
+            return keep.tile(shape, dtype, name=name, align_bytes=64)
+
+        lst1 = sb_tile("lst1", [P, J // 16], U16)
+        lst2 = sb_tile("lst2", [P, J // 16], U16)
+        lst3 = sb_tile("lst3", [P, O // 16], U16)
+        lst4 = sb_tile("lst4", [P, O // 16], U16)
+        lst5 = sb_tile("lst5", [P, O // 16], U16)
+        lst6 = sb_tile("lst6", [P, O // 16], U16)
+        xt_w = sb_tile("xt_w", [P, T], U32)
+        xo_w = sb_tile("xo_w", [P, Z], U16)
+        xt_s = sb_tile("xt_s", [P, T], U8)
+        xo_s = sb_tile("xo_s", [P, Z], U8)
+        w_raw = sb_tile("w_raw", [P, R], U16)
+        w0_raw = sb_tile("w0_raw", [P, R], U32)
+        stage = sb_tile("stage", [PACK, QUADS, 2 * R // 4], I32)
+        s1_raw = sb_tile("s1_raw", [P, 2 * R], U8)
+        wb_w = sb_tile("wb_w", [P, N], U32)
+        ws_w = sb_tile("ws_w", [P, N], U32)
+        s2 = sb_tile("s2", [P, 2 * N], U8)
+        fa = sb_tile("fa", [P, PACK], F32)
+        fb = sb_tile("fb", [P, PACK], F32)
+        fd = sb_tile("fd", [P, PACK], F32)
+
+        def words4(src):
+            return src[0].rearrange("p n t -> p (n t)").bitcast(I32)
+
+        def load_words(eng, tile, src):
+            eng.dma_start(out=tile[:].bitcast(I32), in_=src)
+
+        def load_stage(eng, slot, src):
+            eng.dma_start(
+                out=stage[:, :, slot * (R // 4) : (slot + 1) * (R // 4)],
+                in_=src[0].bitcast(I32).rearrange("(q r) c -> r q c", r=PACK),
+            )
+
+        def load_window_rows(eng, tile, src, q):
+            rows = src[0, PACK * q : PACK * (q + 1), :].bitcast(I32)
+            eng.dma_start(
+                out=tile[QUAD * q : QUAD * (q + 1), :].bitcast(I32),
+                in_=rows.partition_broadcast(QUAD // PACK),
+            )
+
+        def load_plane_rows(eng, slot, src, q):
+            eng.dma_start(
+                out=s2[QUAD * q : QUAD * q + PACK, slot * N : (slot + 1) * N].bitcast(I32),
+                in_=src[0, PACK * q : PACK * (q + 1), :].bitcast(I32),
+            )
+
+        nc.vector.memset(s1_raw[:].bitcast(I32), 0)
+        nc.vector.memset(s2[:].bitcast(I32), 0)
+
+        nc.sync.dma_start(lst2[:], offs2)
+        load_stage(nc.scalar, 0, w0_scales)
+        load_window_rows(nc.gpsimd, xt_s, xt_scales, 2)
+        nc.sync.dma_start(lst1[:], offs)
+        load_stage(nc.scalar, 1, w_scales)
+        load_words(nc.sync, xo_w, xo_words[0].bitcast(I32))
+        load_window_rows(nc.scalar, xo_s, xo_scales, 0)
+        load_words(nc.sync, xt_w, words4(xt_words))
+        load_window_rows(nc.scalar, xo_s, xo_scales, 1)
+        load_window_rows(nc.gpsimd, xt_s, xt_scales, 3)
+        load_words(nc.sync, w0_raw, words4(w0_words))
+        load_window_rows(nc.scalar, xo_s, xo_scales, 2)
+        load_words(nc.sync, w_raw, w_words[0].bitcast(I32))
+        load_window_rows(nc.scalar, xo_s, xo_scales, 3)
+        nc.sync.dma_start(lst3[:], offs3)
+        load_window_rows(nc.scalar, xt_s, xt_scales, 0)
+        nc.sync.dma_start(lst4[:], offs4)
+        load_window_rows(nc.scalar, xt_s, xt_scales, 1)
+        nc.sync.dma_start(lst5[:], offs5)
+        nc.sync.dma_start(lst6[:], offs6)
+        for tile, src in ((fa, sa), (fb, sb), (fd, sd)):
+            nc.sync.dma_start(out=tile[:], in_=src.rearrange("(p t) o -> p (t o)", t=PACK))
+        load_words(nc.sync, ws_w, words4(ws_words))
+        for q in range(QUADS):
+            load_plane_rows(nc.sync, 0, ws_scales, q)
+        load_words(nc.sync, wb_w, words4(wb_words))
+        for q in range(QUADS):
+            load_plane_rows(nc.sync, 1, wb_scales, q)
+
+        for q in range(QUADS):
+            nc.vector.tensor_copy(out=s1_raw[QUAD * q : QUAD * q + PACK, :].bitcast(I32), in_=stage[:, q, :])
+        s1 = sb_tile("s1", [P, 2, PACK, P], U8)
+        for t in range(PACK):
+            nc.gpsimd.tensor_copy(
+                out=s1[:, :, t, :],
+                in_=s1_raw[:].rearrange("p (i m t) -> p i t m", i=2, t=PACK)[:, :, t, :],
+            )
+
+        w0_p = sb_tile("w0_p", [P, PACK, P], U32)
+        nc.scalar.copy(out=w0_p[:].rearrange("p t m -> p m t"), in_=w0_raw[:].rearrange("p (m t) -> p m t", t=PACK))
+        w_p = sb_tile("w_p", [P, PACK, P], U16)
+        nc.scalar.copy(out=w_p[:], in_=w_raw[:].rearrange("p (m t) -> p t m", t=PACK))
+
+        og_w = sb_tile("og_w", [P, J], U16)
+        og_s = sb_tile("og_s", [P, J], U8)
+        tg_w = sb_tile("tg_w", [P, J], U32)
+        tg_s = sb_tile("tg_s", [P, J], U8)
+        nc.vector.tensor_copy(out=og_w[:], in_=xo_w[:].indirect(lst2[:]))
+        nc.vector.tensor_copy(out=og_s[:], in_=xo_s[:].indirect(lst2[:]))
+        nc.vector.tensor_copy(out=tg_w[:], in_=xt_w[:].indirect(lst1[:]))
+        nc.vector.tensor_copy(out=tg_s[:], in_=xt_s[:].indirect(lst1[:]))
+
+        rows_a = []
+        for t in range(PACK):
+            acc = psum.tile([P, J], F32, name=f"acc{t}")
+            nc.tensor.matmul_mx(
+                out=acc[:], lhsT=w0_p[:, t, :].bitcast(E5M2), lhsT_scale=s1[:, 0, t, :],
+                rhs=og_w[:].bitcast(E2M1), rhs_scale=og_s[:], start=True, stop=False,
+            )
+            nc.tensor.matmul_mx(
+                out=acc[:], lhsT=w_p[:, t, :].bitcast(E2M1), lhsT_scale=s1[:, 1, t, :],
+                rhs=tg_w[:].bitcast(E4M3), rhs_scale=tg_s[:], start=False, stop=True,
+            )
+            a_t = sb_tile(f"a{t}", [P, J], F32)
+            nc.vector.tensor_copy(out=a_t[:], in_=acc[:])
+            rows_a.append(a_t)
+
+        x6_w = sb_tile("x6_w", [P, O], U32)
+        x6_s = sb_tile("x6_s", [P, O], U8)
+        nc.vector.tensor_copy(out=x6_w[:], in_=xt_w[:].indirect(lst6[:]))
+        nc.vector.tensor_copy(out=x6_s[:], in_=xt_s[:].indirect(lst6[:]))
+        ys = []
+        for h in range(N // P):
+            y = psum.tile([P, O], F32, name=f"y{h}")
+            nc.tensor.matmul_mx(
+                out=y[:], lhsT=ws_w[:, h * P : (h + 1) * P].bitcast(E5M2), lhsT_scale=s2[:, h * P : (h + 1) * P],
+                rhs=x6_w[:].bitcast(E4M3), rhs_scale=x6_s[:], start=True, stop=False,
+            )
+            ys.append(y)
+
+        total = sb_tile("total", [P, PACK, O], F32)
+        for t in range(PACK):
+            ga = sb_tile(f"ga{t}", [P, O], F32)
+            gb = sb_tile(f"gb{t}", [P, O], F32)
+            gd = sb_tile(f"gd{t}", [P, O], F32)
+            part = sb_tile(f"part{t}", [P, O], F32)
+            nc.scalar.activation(out=ga[:], in_=rows_a[t][:].indirect(lst3[:]), func=ACT.Copy, scale=fa[:, t : t + 1])
+            nc.scalar.activation(out=gb[:], in_=rows_a[t][:].indirect(lst4[:]), func=ACT.Copy, scale=fb[:, t : t + 1])
+            nc.vector.tensor_tensor(out=part[:], in0=ga[:], in1=gb[:], op=ALU.add)
+            nc.scalar.activation(out=gd[:], in_=rows_a[t][:].indirect(lst5[:]), func=ACT.Copy, scale=fd[:, t : t + 1])
+            nc.vector.tensor_tensor(out=total[:, t, :], in0=part[:], in1=gd[:], op=ALU.add)
+
+        hid = sb_tile("hid", [P, O, PACK], BF16)
+        nc.vector.tensor_scalar(
+            out=hid[:], in0=total[:].rearrange("p t o -> p o t"), scalar1=0.0, scalar2=None, op0=ALU.max
+        )
+        hq_w = sb_tile("hq_w", [P, O], U32)
+        hq_s = sb_tile("hq_s", [P, O], U8)
+        nc.vector.quantize_mx(out=hq_w[:].bitcast(E4M3), scales=hq_s[:], in_=hid[:].rearrange("p o t -> p (o t)"))
+
+        for h in range(N // P):
+            nc.tensor.matmul_mx(
+                out=ys[h][:], lhsT=wb_w[:, h * P : (h + 1) * P].bitcast(E5M2),
+                lhsT_scale=s2[:, N + h * P : N + (h + 1) * P],
+                rhs=hq_w[:].bitcast(E4M3), rhs_scale=hq_s[:], start=False, stop=True,
+            )
+        res0 = sb_tile("res0", [P, O], F32)
+        res1 = sb_tile("res1", [P, O], F32)
+        nc.vector.tensor_copy(out=res0[:], in_=ys[0][:])
+        nc.sync.dma_start(out=out[0:P, :], in_=res0[:])
+        nc.scalar.copy(out=res1[:], in_=ys[1][:])
+        nc.scalar.dma_start(out=out[P : 2 * P, :], in_=res1[:])

@@ -44,7 +44,7 @@ def tile_list_tripleblend_bank_further_plain_kernel(
         xt_w = sb_tile("xt_w", [P, T], U32)
         xo_w = sb_tile("xo_w", [P, Z], U16)
         xt_s = sb_tile("xt_s", [P, T], U8)
-        xo_s = sb_tile("xo_s", [P, Z], U8)
+        xo_s = keep.tile([P, Z], U8, name="xo_s", tag="xo_s", align_bytes=64)
         w_raw = sb_tile("w_raw", [P, R], U16)
         w0_raw = sb_tile("w0_raw", [P, R], U32)
         stage = sb_tile("stage", [PACK, QUADS, 2 * R // 4], I32)
@@ -69,6 +69,12 @@ def tile_list_tripleblend_bank_further_plain_kernel(
             )
 
         def load_window_rows(eng, tile, src, q):
+            eng.dma_start(
+                out=tile[QUAD * q : QUAD * q + PACK, :].bitcast(I32),
+                in_=src[0, PACK * q : PACK * (q + 1), :].bitcast(I32),
+            )
+
+        def load_window_quadrant(eng, tile, src, q):
             rows = src[0, PACK * q : PACK * (q + 1), :].bitcast(I32)
             eng.dma_start(
                 out=tile[QUAD * q : QUAD * (q + 1), :].bitcast(I32),
@@ -84,28 +90,32 @@ def tile_list_tripleblend_bank_further_plain_kernel(
         nc.vector.memset(s1_raw[:].bitcast(I32), 0)
         nc.vector.memset(s2[:].bitcast(I32), 0)
 
-        nc.sync.dma_start(lst2[:], offs2)
-        load_stage(nc.scalar, 0, w0_scales)
-        load_window_rows(nc.gpsimd, xt_s, xt_scales, 2)
+        def load_factor(eng, tile, src):
+            eng.dma_start(out=tile[:], in_=src.rearrange("(p t) o -> p (t o)", t=PACK))
+
+        load_stage(nc.sync, 1, w_scales)
+        load_stage(nc.sync, 0, w0_scales)
+        load_window_quadrant(nc.gpsimd, xo_s, xo_scales, 2)
+        load_window_quadrant(nc.gpsimd, xo_s, xo_scales, 3)
+        load_factor(nc.gpsimd, fd, sd)
         nc.sync.dma_start(lst1[:], offs)
-        load_stage(nc.scalar, 1, w_scales)
-        load_words(nc.sync, xo_w, xo_words[0].bitcast(I32))
-        load_window_rows(nc.scalar, xo_s, xo_scales, 0)
+        nc.sync.dma_start(lst2[:], offs2)
+        load_window_quadrant(nc.sync, xt_s, xt_scales, 0)
+        load_window_quadrant(nc.sync, xt_s, xt_scales, 1)
         load_words(nc.sync, xt_w, words4(xt_words))
-        load_window_rows(nc.scalar, xo_s, xo_scales, 1)
-        load_window_rows(nc.gpsimd, xt_s, xt_scales, 3)
-        load_words(nc.sync, w0_raw, words4(w0_words))
-        load_window_rows(nc.scalar, xo_s, xo_scales, 2)
+        load_words(nc.sync, xo_w, xo_words[0].bitcast(I32))
+        load_window_quadrant(nc.sync, xt_s, xt_scales, 2)
+        load_window_quadrant(nc.sync, xt_s, xt_scales, 3)
+        load_window_quadrant(nc.sync, xo_s, xo_scales, 0)
+        load_window_quadrant(nc.sync, xo_s, xo_scales, 1)
         load_words(nc.sync, w_raw, w_words[0].bitcast(I32))
-        load_window_rows(nc.scalar, xo_s, xo_scales, 3)
+        load_words(nc.sync, w0_raw, words4(w0_words))
         nc.sync.dma_start(lst3[:], offs3)
-        load_window_rows(nc.scalar, xt_s, xt_scales, 0)
+        load_factor(nc.sync, fa, sa)
         nc.sync.dma_start(lst4[:], offs4)
-        load_window_rows(nc.scalar, xt_s, xt_scales, 1)
+        load_factor(nc.sync, fb, sb)
         nc.sync.dma_start(lst5[:], offs5)
         nc.sync.dma_start(lst6[:], offs6)
-        for tile, src in ((fa, sa), (fb, sb), (fd, sd)):
-            nc.sync.dma_start(out=tile[:], in_=src.rearrange("(p t) o -> p (t o)", t=PACK))
         load_words(nc.sync, ws_w, words4(ws_words))
         for q in range(QUADS):
             load_plane_rows(nc.sync, 0, ws_scales, q)
@@ -115,44 +125,56 @@ def tile_list_tripleblend_bank_further_plain_kernel(
 
         for q in range(QUADS):
             nc.vector.tensor_copy(out=s1_raw[QUAD * q : QUAD * q + PACK, :].bitcast(I32), in_=stage[:, q, :])
-        s1 = sb_tile("s1", [P, 2, PACK, P], U8)
-        for t in range(PACK):
-            nc.gpsimd.tensor_copy(
-                out=s1[:, :, t, :],
-                in_=s1_raw[:].rearrange("p (i m t) -> p i t m", i=2, t=PACK)[:, :, t, :],
-            )
+        s1_first = sb_tile("s1_first", [P, 2, P], U8)
+        s1_view = s1_raw[:].rearrange("p (i m t) -> p t i m", i=2, t=PACK)
+        nc.vector.tensor_copy(out=s1_first[:], in_=s1_view[:, 0])
 
-        w0_p = sb_tile("w0_p", [P, PACK, P], U32)
-        nc.scalar.copy(out=w0_p[:].rearrange("p t m -> p m t"), in_=w0_raw[:].rearrange("p (m t) -> p m t", t=PACK))
         w_p = sb_tile("w_p", [P, PACK, P], U16)
-        nc.scalar.copy(out=w_p[:], in_=w_raw[:].rearrange("p (m t) -> p t m", t=PACK))
+        w0_p = sb_tile("w0_p", [P, PACK, P], U32)
+        w_view = w_raw[:].rearrange("p (m t) -> p t m", t=PACK)
+        w0_view = w0_raw[:].rearrange("p (m t) -> p m t", t=PACK)
+        nc.scalar.copy(out=w_p[:, 0, :], in_=w_view[:, 0, :])
+        nc.scalar.copy(out=w0_p[:, 0, :], in_=w0_view[:, :, 0])
+        nc.scalar.copy(out=w_p[:, 1:PACK, :], in_=w_view[:, 1:PACK, :])
+        nc.scalar.copy(out=w0_p[:, 1:PACK, :].rearrange("p t m -> p m t"), in_=w0_view[:, :, 1:PACK])
 
         og_w = sb_tile("og_w", [P, J], U16)
         og_s = sb_tile("og_s", [P, J], U8)
-        tg_w = sb_tile("tg_w", [P, J], U32)
-        tg_s = sb_tile("tg_s", [P, J], U8)
-        nc.vector.tensor_copy(out=og_w[:], in_=xo_w[:].indirect(lst2[:]))
-        nc.vector.tensor_copy(out=og_s[:], in_=xo_s[:].indirect(lst2[:]))
+        tg_w = keep.tile([P, J], U32, name="tg_w", tag="tg_w", align_bytes=64)
+        tg_s = keep.tile([P, J], U8, name="tg_s", tag="tg_s", align_bytes=64)
         nc.vector.tensor_copy(out=tg_w[:], in_=xt_w[:].indirect(lst1[:]))
+        nc.vector.tensor_copy(out=og_w[:], in_=xo_w[:].indirect(lst2[:]))
         nc.vector.tensor_copy(out=tg_s[:], in_=xt_s[:].indirect(lst1[:]))
+        for u in range(2):
+            nc.vector.tensor_copy(out=og_s[:, u * P : (u + 1) * P], in_=xo_s[:].indirect(lst2[:, u * 8 : (u + 1) * 8]))
+        s1_rest = keep.tile([P, PACK - 1, 2, P], U8, name="s1_rest", tag="xo_s", align_bytes=64)
+        for t in range(1, PACK):
+            nc.vector.tensor_copy(out=s1_rest[:, t - 1], in_=s1_view[:, t])
+        s1 = [s1_first[:]] + [s1_rest[:, t - 1] for t in range(1, PACK)]
 
-        rows_a = []
-        for t in range(PACK):
+        def first_stage(t, acc, cols):
+            nc.tensor.matmul_mx(
+                out=acc[:], lhsT=w_p[:, t, :].bitcast(E2M1), lhsT_scale=s1[t][:, 1, :],
+                rhs=tg_w[:, cols].bitcast(E4M3), rhs_scale=tg_s[:, cols], start=True, stop=False,
+            )
+            nc.tensor.matmul_mx(
+                out=acc[:], lhsT=w0_p[:, t, :].bitcast(E5M2), lhsT_scale=s1[t][:, 0, :],
+                rhs=og_w[:, cols].bitcast(E2M1), rhs_scale=og_s[:, cols], start=False, stop=True,
+            )
+
+        rows_a = [sb_tile(f"a{t}", [P, J], F32) for t in range(PACK)]
+        for u in range(2):
+            cols = slice(u * P, (u + 1) * P)
+            acc = psum.tile([P, P], F32, name=f"acc0_{u}")
+            first_stage(0, acc, cols)
+            nc.scalar.copy(out=rows_a[0][:, cols], in_=acc[:])
+        for t in range(1, PACK):
             acc = psum.tile([P, J], F32, name=f"acc{t}")
-            nc.tensor.matmul_mx(
-                out=acc[:], lhsT=w0_p[:, t, :].bitcast(E5M2), lhsT_scale=s1[:, 0, t, :],
-                rhs=og_w[:].bitcast(E2M1), rhs_scale=og_s[:], start=True, stop=False,
-            )
-            nc.tensor.matmul_mx(
-                out=acc[:], lhsT=w_p[:, t, :].bitcast(E2M1), lhsT_scale=s1[:, 1, t, :],
-                rhs=tg_w[:].bitcast(E4M3), rhs_scale=tg_s[:], start=False, stop=True,
-            )
-            a_t = sb_tile(f"a{t}", [P, J], F32)
-            nc.vector.tensor_copy(out=a_t[:], in_=acc[:])
-            rows_a.append(a_t)
+            first_stage(t, acc, slice(0, J))
+            nc.vector.tensor_copy(out=rows_a[t][:], in_=acc[:])
 
-        x6_w = sb_tile("x6_w", [P, O], U32)
-        x6_s = sb_tile("x6_s", [P, O], U8)
+        x6_w = keep.tile([P, O], U32, name="x6_w", tag="tg_w", align_bytes=64)
+        x6_s = keep.tile([P, O], U8, name="x6_s", tag="tg_s", align_bytes=64)
         nc.vector.tensor_copy(out=x6_w[:], in_=xt_w[:].indirect(lst6[:]))
         nc.vector.tensor_copy(out=x6_s[:], in_=xt_s[:].indirect(lst6[:]))
         ys = []
@@ -164,25 +186,43 @@ def tile_list_tripleblend_bank_further_plain_kernel(
             )
             ys.append(y)
 
-        total = sb_tile("total", [P, PACK, O], F32)
+        half = O // 2
+        totals = [sb_tile(f"total{u}", [P, PACK, half], F32) for u in range(2)]
         for t in range(PACK):
             ga = sb_tile(f"ga{t}", [P, O], F32)
             gb = sb_tile(f"gb{t}", [P, O], F32)
-            gd = sb_tile(f"gd{t}", [P, O], F32)
             part = sb_tile(f"part{t}", [P, O], F32)
             nc.scalar.activation(out=ga[:], in_=rows_a[t][:].indirect(lst3[:]), func=ACT.Copy, scale=fa[:, t : t + 1])
             nc.scalar.activation(out=gb[:], in_=rows_a[t][:].indirect(lst4[:]), func=ACT.Copy, scale=fb[:, t : t + 1])
             nc.vector.tensor_tensor(out=part[:], in0=ga[:], in1=gb[:], op=ALU.add)
-            nc.scalar.activation(out=gd[:], in_=rows_a[t][:].indirect(lst5[:]), func=ACT.Copy, scale=fd[:, t : t + 1])
-            nc.vector.tensor_tensor(out=total[:, t, :], in0=part[:], in1=gd[:], op=ALU.add)
+            if t < PACK - 1:
+                gd = sb_tile(f"gd{t}", [P, O], F32)
+                nc.scalar.activation(out=gd[:], in_=rows_a[t][:].indirect(lst5[:]), func=ACT.Copy, scale=fd[:, t : t + 1])
+                for u in range(2):
+                    cols = slice(u * half, (u + 1) * half)
+                    nc.vector.tensor_tensor(out=totals[u][:, t, :], in0=part[:, cols], in1=gd[:, cols], op=ALU.add)
+            else:
+                for u in range(2):
+                    cols = slice(u * half, (u + 1) * half)
+                    gd = sb_tile(f"gd{t}_{u}", [P, half], F32)
+                    nc.scalar.activation(
+                        out=gd[:], in_=rows_a[t][:].indirect(lst5[:, u * half // 16 : (u + 1) * half // 16]),
+                        func=ACT.Copy, scale=fd[:, t : t + 1],
+                    )
+                    nc.vector.tensor_tensor(out=totals[u][:, t, :], in0=part[:, cols], in1=gd[:], op=ALU.add)
 
-        hid = sb_tile("hid", [P, O, PACK], BF16)
-        nc.vector.tensor_scalar(
-            out=hid[:], in0=total[:].rearrange("p t o -> p o t"), scalar1=0.0, scalar2=None, op0=ALU.max
-        )
         hq_w = sb_tile("hq_w", [P, O], U32)
         hq_s = sb_tile("hq_s", [P, O], U8)
-        nc.vector.quantize_mx(out=hq_w[:].bitcast(E4M3), scales=hq_s[:], in_=hid[:].rearrange("p o t -> p (o t)"))
+        hids = [sb_tile(f"hid{u}", [P, half, PACK], BF16) for u in range(2)]
+        for u in range(2):
+            nc.vector.tensor_scalar(
+                out=hids[u][:], in0=totals[u][:].rearrange("p t o -> p o t"), scalar1=0.0, scalar2=None, op0=ALU.max
+            )
+        for u in range(2):
+            cols = slice(u * half, (u + 1) * half)
+            nc.vector.quantize_mx(
+                out=hq_w[:, cols].bitcast(E4M3), scales=hq_s[:, cols], in_=hids[u][:].rearrange("p o t -> p (o t)")
+            )
 
         for h in range(N // P):
             nc.tensor.matmul_mx(

@@ -87,6 +87,8 @@ def tile_list_tripleblend_bank_further_plain_kernel(
                 in_=src[0, PACK * q : PACK * (q + 1), :].bitcast(I32),
             )
 
+        nc.vector.memset(xt_s[0 : 2 * QUAD, :].bitcast(I32), 0)
+        nc.vector.memset(xo_s[2 * QUAD : P, :].bitcast(I32), 0)
         nc.vector.memset(s1_raw[:].bitcast(I32), 0)
         nc.vector.memset(s2[:].bitcast(I32), 0)
 
@@ -95,26 +97,26 @@ def tile_list_tripleblend_bank_further_plain_kernel(
 
         load_stage(nc.sync, 1, w_scales)
         load_stage(nc.sync, 0, w0_scales)
-        load_window_quadrant(nc.gpsimd, xo_s, xo_scales, 2)
-        load_window_quadrant(nc.gpsimd, xo_s, xo_scales, 3)
-        load_factor(nc.gpsimd, fd, sd)
+        load_window_quadrant(nc.gpsimd, xo_s, xo_scales, 0)
+        load_window_quadrant(nc.gpsimd, xo_s, xo_scales, 1)
+        load_factor(nc.gpsimd, fa, sa)
+        load_factor(nc.gpsimd, fb, sb)
         nc.sync.dma_start(lst1[:], offs)
         nc.sync.dma_start(lst2[:], offs2)
-        load_window_quadrant(nc.sync, xt_s, xt_scales, 0)
-        load_window_quadrant(nc.sync, xt_s, xt_scales, 1)
-        load_words(nc.sync, xt_w, words4(xt_words))
-        load_words(nc.sync, xo_w, xo_words[0].bitcast(I32))
         load_window_quadrant(nc.sync, xt_s, xt_scales, 2)
         load_window_quadrant(nc.sync, xt_s, xt_scales, 3)
-        load_window_quadrant(nc.sync, xo_s, xo_scales, 0)
-        load_window_quadrant(nc.sync, xo_s, xo_scales, 1)
+        load_words(nc.sync, xt_w, words4(xt_words))
+        load_words(nc.sync, xo_w, xo_words[0].bitcast(I32))
+        load_window_rows(nc.sync, xt_s, xt_scales, 0)
+        load_window_rows(nc.sync, xt_s, xt_scales, 1)
+        load_window_rows(nc.sync, xo_s, xo_scales, 2)
+        load_window_rows(nc.sync, xo_s, xo_scales, 3)
         load_words(nc.sync, w_raw, w_words[0].bitcast(I32))
         load_words(nc.sync, w0_raw, words4(w0_words))
         nc.sync.dma_start(lst3[:], offs3)
-        load_factor(nc.sync, fa, sa)
         nc.sync.dma_start(lst4[:], offs4)
-        load_factor(nc.sync, fb, sb)
         nc.sync.dma_start(lst5[:], offs5)
+        load_factor(nc.sync, fd, sd)
         nc.sync.dma_start(lst6[:], offs6)
         load_words(nc.sync, ws_w, words4(ws_words))
         for q in range(QUADS):
@@ -234,5 +236,5 @@ def tile_list_tripleblend_bank_further_plain_kernel(
         res1 = sb_tile("res1", [P, O], F32)
         nc.vector.tensor_copy(out=res0[:], in_=ys[0][:])
         nc.sync.dma_start(out=out[0:P, :], in_=res0[:])
-        nc.scalar.copy(out=res1[:], in_=ys[1][:])
-        nc.scalar.dma_start(out=out[P : 2 * P, :], in_=res1[:])
+        nc.vector.tensor_copy(out=res1[:], in_=ys[1][:])
+        nc.sync.dma_start(out=out[P : 2 * P, :], in_=res1[:])

@@ -21,6 +21,13 @@ P = 128
 PACK = 4
 QUADS = 4
 QUAD = 32
+SCALE_ROWS = 4
+PER_COLUMN = 16
+WORD = 4
+HALVES = 2
+SLOT_W0, SLOT_W = 0, 1
+SLOT_WS, SLOT_WB = 0, 1
+EARLY_TILES = 2
 
 
 def tile_list_tripleblend_bank_further_plain_kernel(
@@ -32,107 +39,102 @@ def tile_list_tripleblend_bank_further_plain_kernel(
         keep = ctx.enter_context(tc.tile_pool(name="keep", bufs=1))
         psum = ctx.enter_context(tc.psum_pool(name="psum", bufs=1))
 
-        def sb_tile(name, shape, dtype):
+        def new_tile(name, shape, dtype):
             return keep.tile(shape, dtype, name=name, align_bytes=64)
 
-        lst1 = sb_tile("lst1", [P, J // 16], U16)
-        lst2 = sb_tile("lst2", [P, J // 16], U16)
-        lst3 = sb_tile("lst3", [P, O // 16], U16)
-        lst4 = sb_tile("lst4", [P, O // 16], U16)
-        lst5 = sb_tile("lst5", [P, O // 16], U16)
-        lst6 = sb_tile("lst6", [P, O // 16], U16)
-        xt_w = sb_tile("xt_w", [P, T], U32)
-        xo_w = sb_tile("xo_w", [P, Z], U16)
-        xt_s = sb_tile("xt_s", [P, T], U8)
-        xo_s = keep.tile([P, Z], U8, name="xo_s", tag="xo_s", align_bytes=64)
-        w_raw = sb_tile("w_raw", [P, R], U16)
-        w0_raw = sb_tile("w0_raw", [P, R], U32)
-        stage = sb_tile("stage", [PACK, QUADS, 2 * R // 4], I32)
-        s1_raw = sb_tile("s1_raw", [P, 2 * R], U8)
-        wb_w = sb_tile("wb_w", [P, N], U32)
-        ws_w = sb_tile("ws_w", [P, N], U32)
-        s2 = sb_tile("s2", [P, 2 * N], U8)
-        fa = sb_tile("fa", [P, PACK], F32)
-        fb = sb_tile("fb", [P, PACK], F32)
-        fd = sb_tile("fd", [P, PACK], F32)
+        def tile_in(buffer, name, shape, dtype):
+            return keep.tile(shape, dtype, name=name, tag=buffer, align_bytes=64)
 
-        def words4(src):
-            return src[0].rearrange("p n t -> p (n t)").bitcast(I32)
+        lst1 = new_tile("lst1", [P, J // PER_COLUMN], U16)
+        lst2 = new_tile("lst2", [P, J // PER_COLUMN], U16)
+        lst3 = new_tile("lst3", [P, O // PER_COLUMN], U16)
+        lst4 = new_tile("lst4", [P, O // PER_COLUMN], U16)
+        lst5 = new_tile("lst5", [P, O // PER_COLUMN], U16)
+        lst6 = new_tile("lst6", [P, O // PER_COLUMN], U16)
+        xt_w = new_tile("xt_w", [P, T], U32)
+        xo_w = new_tile("xo_w", [P, Z], U16)
+        xt_s = new_tile("xt_s", [P, T], U8)
+        xo_s = tile_in("xo_s", "xo_s", [P, Z], U8)
+        w_raw = new_tile("w_raw", [P, R], U16)
+        w0_raw = new_tile("w0_raw", [P, R], U32)
+        stage = new_tile("stage", [SCALE_ROWS, QUADS, 2 * R // WORD], I32)
+        s1_raw = new_tile("s1_raw", [P, 2 * R], U8)
+        wb_w = new_tile("wb_w", [P, N], U32)
+        ws_w = new_tile("ws_w", [P, N], U32)
+        s2 = new_tile("s2", [P, 2 * N], U8)
+        fa = new_tile("fa", [P, PACK], F32)
+        fb = new_tile("fb", [P, PACK], F32)
+        fd = new_tile("fd", [P, PACK], F32)
 
-        def load_words(eng, tile, src):
-            eng.dma_start(out=tile[:].bitcast(I32), in_=src)
+        def load_fp8_words(tile, src):
+            nc.sync.dma_start(out=tile[:].bitcast(I32), in_=src[0].rearrange("p n t -> p (n t)").bitcast(I32))
 
-        def load_stage(eng, slot, src):
-            eng.dma_start(
-                out=stage[:, :, slot * (R // 4) : (slot + 1) * (R // 4)],
-                in_=src[0].bitcast(I32).rearrange("(q r) c -> r q c", r=PACK),
+        def load_fp4_words(tile, src):
+            nc.sync.dma_start(out=tile[:].bitcast(I32), in_=src[0].bitcast(I32))
+
+        def scale_rows(src, q):
+            return src[0, SCALE_ROWS * q : SCALE_ROWS * (q + 1), :].bitcast(I32)
+
+        def load_staged(slot, src):
+            nc.sync.dma_start(
+                out=stage[:, :, slot * (R // WORD) : (slot + 1) * (R // WORD)],
+                in_=src[0].bitcast(I32).rearrange("(q i) c -> i q c", i=SCALE_ROWS),
             )
 
-        def load_window_rows(eng, tile, src, q):
-            eng.dma_start(
-                out=tile[QUAD * q : QUAD * q + PACK, :].bitcast(I32),
-                in_=src[0, PACK * q : PACK * (q + 1), :].bitcast(I32),
+        def load_rows(plane, src, q):
+            nc.sync.dma_start(out=plane[QUAD * q : QUAD * q + SCALE_ROWS, :].bitcast(I32), in_=scale_rows(src, q))
+
+        def load_quadrant(engine, plane, src, q):
+            engine.dma_start(
+                out=plane[QUAD * q : QUAD * (q + 1), :].bitcast(I32),
+                in_=scale_rows(src, q).partition_broadcast(QUAD // SCALE_ROWS),
             )
 
-        def load_window_quadrant(eng, tile, src, q):
-            rows = src[0, PACK * q : PACK * (q + 1), :].bitcast(I32)
-            eng.dma_start(
-                out=tile[QUAD * q : QUAD * (q + 1), :].bitcast(I32),
-                in_=rows.partition_broadcast(QUAD // PACK),
-            )
-
-        def load_plane_rows(eng, slot, src, q):
-            eng.dma_start(
-                out=s2[QUAD * q : QUAD * q + PACK, slot * N : (slot + 1) * N].bitcast(I32),
-                in_=src[0, PACK * q : PACK * (q + 1), :].bitcast(I32),
-            )
+        def load_factor(engine, tile, src):
+            engine.dma_start(out=tile[:], in_=src.rearrange("(p t) o -> p (t o)", t=PACK))
 
         nc.vector.memset(xt_s[0 : 2 * QUAD, :].bitcast(I32), 0)
         nc.vector.memset(xo_s[2 * QUAD : P, :].bitcast(I32), 0)
         nc.vector.memset(s1_raw[:].bitcast(I32), 0)
         nc.vector.memset(s2[:].bitcast(I32), 0)
 
-        def load_factor(eng, tile, src):
-            eng.dma_start(out=tile[:], in_=src.rearrange("(p t) o -> p (t o)", t=PACK))
-
-        load_stage(nc.sync, 1, w_scales)
-        load_stage(nc.sync, 0, w0_scales)
-        load_window_quadrant(nc.gpsimd, xo_s, xo_scales, 0)
-        load_window_quadrant(nc.gpsimd, xo_s, xo_scales, 1)
+        load_staged(SLOT_W, w_scales)
+        load_staged(SLOT_W0, w0_scales)
+        load_quadrant(nc.gpsimd, xo_s, xo_scales, 0)
+        load_quadrant(nc.gpsimd, xo_s, xo_scales, 1)
         load_factor(nc.gpsimd, fa, sa)
         load_factor(nc.gpsimd, fb, sb)
         nc.sync.dma_start(lst1[:], offs)
         nc.sync.dma_start(lst2[:], offs2)
-        load_window_quadrant(nc.sync, xt_s, xt_scales, 2)
-        load_window_quadrant(nc.sync, xt_s, xt_scales, 3)
-        load_words(nc.sync, xt_w, words4(xt_words))
-        load_words(nc.sync, xo_w, xo_words[0].bitcast(I32))
-        load_window_rows(nc.sync, xt_s, xt_scales, 0)
-        load_window_rows(nc.sync, xt_s, xt_scales, 1)
-        load_window_rows(nc.sync, xo_s, xo_scales, 2)
-        load_window_rows(nc.sync, xo_s, xo_scales, 3)
-        load_words(nc.sync, w_raw, w_words[0].bitcast(I32))
-        load_words(nc.sync, w0_raw, words4(w0_words))
+        load_quadrant(nc.sync, xt_s, xt_scales, 2)
+        load_quadrant(nc.sync, xt_s, xt_scales, 3)
+        load_fp8_words(xt_w, xt_words)
+        load_fp4_words(xo_w, xo_words)
+        load_rows(xt_s, xt_scales, 0)
+        load_rows(xt_s, xt_scales, 1)
+        load_rows(xo_s, xo_scales, 2)
+        load_rows(xo_s, xo_scales, 3)
+        load_fp4_words(w_raw, w_words)
+        load_fp8_words(w0_raw, w0_words)
         nc.sync.dma_start(lst3[:], offs3)
         nc.sync.dma_start(lst4[:], offs4)
         nc.sync.dma_start(lst5[:], offs5)
         load_factor(nc.sync, fd, sd)
         nc.sync.dma_start(lst6[:], offs6)
-        load_words(nc.sync, ws_w, words4(ws_words))
-        for q in range(QUADS):
-            load_plane_rows(nc.sync, 0, ws_scales, q)
-        load_words(nc.sync, wb_w, words4(wb_words))
-        for q in range(QUADS):
-            load_plane_rows(nc.sync, 1, wb_scales, q)
+        for slot, tile, words, scales in ((SLOT_WS, ws_w, ws_words, ws_scales), (SLOT_WB, wb_w, wb_words, wb_scales)):
+            load_fp8_words(tile, words)
+            for q in range(QUADS):
+                load_rows(s2[:, slot * N : (slot + 1) * N], scales, q)
 
         for q in range(QUADS):
-            nc.vector.tensor_copy(out=s1_raw[QUAD * q : QUAD * q + PACK, :].bitcast(I32), in_=stage[:, q, :])
-        s1_first = sb_tile("s1_first", [P, 2, P], U8)
-        s1_view = s1_raw[:].rearrange("p (i m t) -> p t i m", i=2, t=PACK)
-        nc.vector.tensor_copy(out=s1_first[:], in_=s1_view[:, 0])
+            nc.vector.tensor_copy(out=s1_raw[QUAD * q : QUAD * q + SCALE_ROWS, :].bitcast(I32), in_=stage[:, q, :])
+        s1_view = s1_raw[:].rearrange("p (s m t) -> p t s m", s=2, t=PACK)
+        s1_early = new_tile("s1_early", [P, EARLY_TILES, 2, P], U8)
+        for t in range(EARLY_TILES):
+            nc.vector.tensor_copy(out=s1_early[:, t], in_=s1_view[:, t])
 
-        w_p = sb_tile("w_p", [P, PACK, P], U16)
-        w0_p = sb_tile("w0_p", [P, PACK, P], U32)
+        w_p = new_tile("w_p", [P, PACK, P], U16)
+        w0_p = new_tile("w0_p", [P, PACK, P], U32)
         w_view = w_raw[:].rearrange("p (m t) -> p t m", t=PACK)
         w0_view = w0_raw[:].rearrange("p (m t) -> p m t", t=PACK)
         nc.scalar.copy(out=w_p[:, 0, :], in_=w_view[:, 0, :])
@@ -140,101 +142,106 @@ def tile_list_tripleblend_bank_further_plain_kernel(
         nc.scalar.copy(out=w_p[:, 1:PACK, :], in_=w_view[:, 1:PACK, :])
         nc.scalar.copy(out=w0_p[:, 1:PACK, :].rearrange("p t m -> p m t"), in_=w0_view[:, :, 1:PACK])
 
-        og_w = sb_tile("og_w", [P, J], U16)
-        og_s = sb_tile("og_s", [P, J], U8)
-        tg_w = keep.tile([P, J], U32, name="tg_w", tag="tg_w", align_bytes=64)
-        tg_s = keep.tile([P, J], U8, name="tg_s", tag="tg_s", align_bytes=64)
+        j_half = J // HALVES
+        j_cols = [slice(u * j_half, (u + 1) * j_half) for u in range(HALVES)]
+        og_w = new_tile("og_w", [P, J], U16)
+        og_s = new_tile("og_s", [P, J], U8)
+        tg_w = tile_in("tg_w", "tg_w", [P, J], U32)
+        tg_s = tile_in("tg_s", "tg_s", [P, J], U8)
         nc.vector.tensor_copy(out=tg_w[:], in_=xt_w[:].indirect(lst1[:]))
         nc.vector.tensor_copy(out=og_w[:], in_=xo_w[:].indirect(lst2[:]))
         nc.vector.tensor_copy(out=tg_s[:], in_=xt_s[:].indirect(lst1[:]))
-        for u in range(2):
-            nc.vector.tensor_copy(out=og_s[:, u * P : (u + 1) * P], in_=xo_s[:].indirect(lst2[:, u * 8 : (u + 1) * 8]))
-        s1_rest = keep.tile([P, PACK - 1, 2, P], U8, name="s1_rest", tag="xo_s", align_bytes=64)
-        for t in range(1, PACK):
-            nc.vector.tensor_copy(out=s1_rest[:, t - 1], in_=s1_view[:, t])
-        s1 = [s1_first[:]] + [s1_rest[:, t - 1] for t in range(1, PACK)]
+        for u in range(HALVES):
+            entries = lst2[:, u * j_half // PER_COLUMN : (u + 1) * j_half // PER_COLUMN]
+            nc.vector.tensor_copy(out=og_s[:, j_cols[u]], in_=xo_s[:].indirect(entries))
+
+        s1_late = tile_in("xo_s", "s1_late", [P, PACK - EARLY_TILES, 2, P], U8)
+        for t in range(EARLY_TILES, PACK):
+            nc.vector.tensor_copy(out=s1_late[:, t - EARLY_TILES], in_=s1_view[:, t])
+        s1 = [s1_early[:, t] for t in range(EARLY_TILES)] + [s1_late[:, t] for t in range(PACK - EARLY_TILES)]
 
         def first_stage(t, acc, cols):
             nc.tensor.matmul_mx(
-                out=acc[:], lhsT=w_p[:, t, :].bitcast(E2M1), lhsT_scale=s1[t][:, 1, :],
+                out=acc[:], lhsT=w_p[:, t, :].bitcast(E2M1), lhsT_scale=s1[t][:, SLOT_W, :],
                 rhs=tg_w[:, cols].bitcast(E4M3), rhs_scale=tg_s[:, cols], start=True, stop=False,
             )
             nc.tensor.matmul_mx(
-                out=acc[:], lhsT=w0_p[:, t, :].bitcast(E5M2), lhsT_scale=s1[t][:, 0, :],
+                out=acc[:], lhsT=w0_p[:, t, :].bitcast(E5M2), lhsT_scale=s1[t][:, SLOT_W0, :],
                 rhs=og_w[:, cols].bitcast(E2M1), rhs_scale=og_s[:, cols], start=False, stop=True,
             )
 
-        rows_a = [sb_tile(f"a{t}", [P, J], F32) for t in range(PACK)]
-        for u in range(2):
-            cols = slice(u * P, (u + 1) * P)
-            acc = psum.tile([P, P], F32, name=f"acc0_{u}")
-            first_stage(0, acc, cols)
-            nc.scalar.copy(out=rows_a[0][:, cols], in_=acc[:])
+        rows_a = [new_tile(f"a{t}", [P, J], F32) for t in range(PACK)]
+        for u in range(HALVES):
+            acc = psum.tile([P, j_half], F32, name=f"acc0_{u}")
+            first_stage(0, acc, j_cols[u])
+            nc.scalar.copy(out=rows_a[0][:, j_cols[u]], in_=acc[:])
         for t in range(1, PACK):
             acc = psum.tile([P, J], F32, name=f"acc{t}")
             first_stage(t, acc, slice(0, J))
             nc.vector.tensor_copy(out=rows_a[t][:], in_=acc[:])
 
-        x6_w = keep.tile([P, O], U32, name="x6_w", tag="tg_w", align_bytes=64)
-        x6_s = keep.tile([P, O], U8, name="x6_s", tag="tg_s", align_bytes=64)
+        x6_w = tile_in("tg_w", "x6_w", [P, O], U32)
+        x6_s = tile_in("tg_s", "x6_s", [P, O], U8)
         nc.vector.tensor_copy(out=x6_w[:], in_=xt_w[:].indirect(lst6[:]))
         nc.vector.tensor_copy(out=x6_s[:], in_=xt_s[:].indirect(lst6[:]))
-        ys = []
+        sums = []
         for h in range(N // P):
             y = psum.tile([P, O], F32, name=f"y{h}")
             nc.tensor.matmul_mx(
-                out=y[:], lhsT=ws_w[:, h * P : (h + 1) * P].bitcast(E5M2), lhsT_scale=s2[:, h * P : (h + 1) * P],
+                out=y[:], lhsT=ws_w[:, h * P : (h + 1) * P].bitcast(E5M2),
+                lhsT_scale=s2[:, SLOT_WS * N + h * P : SLOT_WS * N + (h + 1) * P],
                 rhs=x6_w[:].bitcast(E4M3), rhs_scale=x6_s[:], start=True, stop=False,
             )
-            ys.append(y)
+            sums.append(y)
 
-        half = O // 2
-        totals = [sb_tile(f"total{u}", [P, PACK, half], F32) for u in range(2)]
+        def look_up(dst, t, entries, factor):
+            nc.scalar.activation(out=dst[:], in_=rows_a[t][:].indirect(entries), func=ACT.Copy, scale=factor[:, t : t + 1])
+
+        o_half = O // HALVES
+        o_cols = [slice(u * o_half, (u + 1) * o_half) for u in range(HALVES)]
+        totals = [new_tile(f"total{u}", [P, PACK, o_half], F32) for u in range(HALVES)]
         for t in range(PACK):
-            ga = sb_tile(f"ga{t}", [P, O], F32)
-            gb = sb_tile(f"gb{t}", [P, O], F32)
-            part = sb_tile(f"part{t}", [P, O], F32)
-            nc.scalar.activation(out=ga[:], in_=rows_a[t][:].indirect(lst3[:]), func=ACT.Copy, scale=fa[:, t : t + 1])
-            nc.scalar.activation(out=gb[:], in_=rows_a[t][:].indirect(lst4[:]), func=ACT.Copy, scale=fb[:, t : t + 1])
+            ga = new_tile(f"ga{t}", [P, O], F32)
+            gb = new_tile(f"gb{t}", [P, O], F32)
+            part = new_tile(f"part{t}", [P, O], F32)
+            look_up(ga, t, lst3[:], fa)
+            look_up(gb, t, lst4[:], fb)
             nc.vector.tensor_tensor(out=part[:], in0=ga[:], in1=gb[:], op=ALU.add)
             if t < PACK - 1:
-                gd = sb_tile(f"gd{t}", [P, O], F32)
-                nc.scalar.activation(out=gd[:], in_=rows_a[t][:].indirect(lst5[:]), func=ACT.Copy, scale=fd[:, t : t + 1])
-                for u in range(2):
-                    cols = slice(u * half, (u + 1) * half)
-                    nc.vector.tensor_tensor(out=totals[u][:, t, :], in0=part[:, cols], in1=gd[:, cols], op=ALU.add)
-            else:
-                for u in range(2):
-                    cols = slice(u * half, (u + 1) * half)
-                    gd = sb_tile(f"gd{t}_{u}", [P, half], F32)
-                    nc.scalar.activation(
-                        out=gd[:], in_=rows_a[t][:].indirect(lst5[:, u * half // 16 : (u + 1) * half // 16]),
-                        func=ACT.Copy, scale=fd[:, t : t + 1],
+                gd = new_tile(f"gd{t}", [P, O], F32)
+                look_up(gd, t, lst5[:], fd)
+                for u in range(HALVES):
+                    nc.vector.tensor_tensor(
+                        out=totals[u][:, t, :], in0=part[:, o_cols[u]], in1=gd[:, o_cols[u]], op=ALU.add
                     )
-                    nc.vector.tensor_tensor(out=totals[u][:, t, :], in0=part[:, cols], in1=gd[:], op=ALU.add)
+            else:
+                for u in range(HALVES):
+                    gd_half = new_tile(f"gd{t}_{u}", [P, o_half], F32)
+                    look_up(gd_half, t, lst5[:, u * o_half // PER_COLUMN : (u + 1) * o_half // PER_COLUMN], fd)
+                    nc.vector.tensor_tensor(
+                        out=totals[u][:, t, :], in0=part[:, o_cols[u]], in1=gd_half[:], op=ALU.add
+                    )
 
-        hq_w = sb_tile("hq_w", [P, O], U32)
-        hq_s = sb_tile("hq_s", [P, O], U8)
-        hids = [sb_tile(f"hid{u}", [P, half, PACK], BF16) for u in range(2)]
-        for u in range(2):
+        hq_w = new_tile("hq_w", [P, O], U32)
+        hq_s = new_tile("hq_s", [P, O], U8)
+        hids = [new_tile(f"hid{u}", [P, o_half, PACK], BF16) for u in range(HALVES)]
+        for u in range(HALVES):
             nc.vector.tensor_scalar(
                 out=hids[u][:], in0=totals[u][:].rearrange("p t o -> p o t"), scalar1=0.0, scalar2=None, op0=ALU.max
             )
-        for u in range(2):
-            cols = slice(u * half, (u + 1) * half)
+        for u in range(HALVES):
             nc.vector.quantize_mx(
-                out=hq_w[:, cols].bitcast(E4M3), scales=hq_s[:, cols], in_=hids[u][:].rearrange("p o t -> p (o t)")
+                out=hq_w[:, o_cols[u]].bitcast(E4M3), scales=hq_s[:, o_cols[u]],
+                in_=hids[u][:].rearrange("p o t -> p (o t)"),
             )
 
         for h in range(N // P):
             nc.tensor.matmul_mx(
-                out=ys[h][:], lhsT=wb_w[:, h * P : (h + 1) * P].bitcast(E5M2),
-                lhsT_scale=s2[:, N + h * P : N + (h + 1) * P],
+                out=sums[h][:], lhsT=wb_w[:, h * P : (h + 1) * P].bitcast(E5M2),
+                lhsT_scale=s2[:, SLOT_WB * N + h * P : SLOT_WB * N + (h + 1) * P],
                 rhs=hq_w[:].bitcast(E4M3), rhs_scale=hq_s[:], start=False, stop=True,
             )
-        res0 = sb_tile("res0", [P, O], F32)
-        res1 = sb_tile("res1", [P, O], F32)
-        nc.vector.tensor_copy(out=res0[:], in_=ys[0][:])
-        nc.sync.dma_start(out=out[0:P, :], in_=res0[:])
-        nc.vector.tensor_copy(out=res1[:], in_=ys[1][:])
-        nc.sync.dma_start(out=out[P : 2 * P, :], in_=res1[:])
+        results = [new_tile(f"res{h}", [P, O], F32) for h in range(N // P)]
+        for h in range(N // P):
+            nc.vector.tensor_copy(out=results[h][:], in_=sums[h][:])
+            nc.sync.dma_start(out=out[h * P : (h + 1) * P, :], in_=results[h][:])

from contextlib import ExitStack

import concourse.mybir as mybir

K, F, T, Z, J, R, O, N = 512, 512, 1024, 1024, 256, 512, 128, 256
FLOPS = 2 * (K * R * J + F * R * J + R * N * O + K * N * O)

F32 = mybir.dt.float32
BF16 = mybir.dt.bfloat16
I32 = mybir.dt.int32
U32 = mybir.dt.uint32
U16 = mybir.dt.uint16
U8 = mybir.dt.uint8
E4M3 = mybir.dt.float8_e4m3fn_x4
E5M2 = mybir.dt.float8_e5m2_x4
E2M1 = mybir.dt.float4_e2m1fn_x4
ALU = mybir.AluOpType
ACT = mybir.ActivationFunctionType

P = 128
PACK = 4
QUADS = 4
QUAD = 32
SCALE_ROWS = 4
PER_COLUMN = 16
WORD = 4
HALVES = 2
SLOT_W0, SLOT_W = 0, 1
SLOT_WS, SLOT_WB = 0, 1
EARLY_TILES = 2


def tile_list_tripleblend_bank_further_plain_kernel(
    tc, xt_words, xt_scales, w_words, w_scales, xo_words, xo_scales, w0_words, w0_scales, sa, sb, sd,
    wb_words, wb_scales, ws_words, ws_scales, offs, offs2, offs3, offs4, offs5, offs6, out,
):
    nc = tc.nc
    with ExitStack() as ctx:
        keep = ctx.enter_context(tc.tile_pool(name="keep", bufs=1))
        psum = ctx.enter_context(tc.psum_pool(name="psum", bufs=1))

        def new_tile(name, shape, dtype):
            return keep.tile(shape, dtype, name=name, align_bytes=64)

        def tile_in(buffer, name, shape, dtype):
            return keep.tile(shape, dtype, name=name, tag=buffer, align_bytes=64)

        lst1 = new_tile("lst1", [P, J // PER_COLUMN], U16)
        lst2 = new_tile("lst2", [P, J // PER_COLUMN], U16)
        lst3 = new_tile("lst3", [P, O // PER_COLUMN], U16)
        lst4 = new_tile("lst4", [P, O // PER_COLUMN], U16)
        lst5 = new_tile("lst5", [P, O // PER_COLUMN], U16)
        lst6 = new_tile("lst6", [P, O // PER_COLUMN], U16)
        xt_w = new_tile("xt_w", [P, T], U32)
        xo_w = new_tile("xo_w", [P, Z], U16)
        xt_s = new_tile("xt_s", [P, T], U8)
        xo_s = tile_in("xo_s", "xo_s", [P, Z], U8)
        w_raw = new_tile("w_raw", [P, R], U16)
        w0_raw = new_tile("w0_raw", [P, R], U32)
        stage = new_tile("stage", [SCALE_ROWS, QUADS, 2 * R // WORD], I32)
        s1_raw = new_tile("s1_raw", [P, 2 * R], U8)
        wb_w = new_tile("wb_w", [P, N], U32)
        ws_w = new_tile("ws_w", [P, N], U32)
        s2 = new_tile("s2", [P, 2 * N], U8)
        fa = new_tile("fa", [P, PACK], F32)
        fb = new_tile("fb", [P, PACK], F32)
        fd = new_tile("fd", [P, PACK], F32)

        def load_fp8_words(tile, src):
            nc.sync.dma_start(out=tile[:].bitcast(I32), in_=src[0].rearrange("p n t -> p (n t)").bitcast(I32))

        def load_fp4_words(tile, src):
            nc.sync.dma_start(out=tile[:].bitcast(I32), in_=src[0].bitcast(I32))

        def scale_rows(src, q):
            return src[0, SCALE_ROWS * q : SCALE_ROWS * (q + 1), :].bitcast(I32)

        def load_staged(slot, src):
            nc.sync.dma_start(
                out=stage[:, :, slot * (R // WORD) : (slot + 1) * (R // WORD)],
                in_=src[0].bitcast(I32).rearrange("(q i) c -> i q c", i=SCALE_ROWS),
            )

        def load_rows(plane, src, q):
            nc.sync.dma_start(out=plane[QUAD * q : QUAD * q + SCALE_ROWS, :].bitcast(I32), in_=scale_rows(src, q))

        def load_quadrant(engine, plane, src, q):
            engine.dma_start(
                out=plane[QUAD * q : QUAD * (q + 1), :].bitcast(I32),
                in_=scale_rows(src, q).partition_broadcast(QUAD // SCALE_ROWS),
            )

        def load_factor(engine, tile, src):
            engine.dma_start(out=tile[:], in_=src.rearrange("(p t) o -> p (t o)", t=PACK))

        nc.vector.memset(xt_s[0 : 2 * QUAD, :].bitcast(I32), 0)
        nc.vector.memset(xo_s[2 * QUAD : P, :].bitcast(I32), 0)
        nc.vector.memset(s1_raw[:].bitcast(I32), 0)
        nc.vector.memset(s2[:].bitcast(I32), 0)

        load_staged(SLOT_W, w_scales)
        load_staged(SLOT_W0, w0_scales)
        load_quadrant(nc.gpsimd, xo_s, xo_scales, 0)
        load_quadrant(nc.gpsimd, xo_s, xo_scales, 1)
        load_factor(nc.gpsimd, fa, sa)
        load_factor(nc.gpsimd, fb, sb)
        nc.sync.dma_start(lst1[:], offs)
        nc.sync.dma_start(lst2[:], offs2)
        load_quadrant(nc.sync, xt_s, xt_scales, 2)
        load_quadrant(nc.sync, xt_s, xt_scales, 3)
        load_fp8_words(xt_w, xt_words)
        load_fp4_words(xo_w, xo_words)
        load_rows(xt_s, xt_scales, 0)
        load_rows(xt_s, xt_scales, 1)
        load_rows(xo_s, xo_scales, 2)
        load_rows(xo_s, xo_scales, 3)
        load_fp4_words(w_raw, w_words)
        load_fp8_words(w0_raw, w0_words)
        nc.sync.dma_start(lst3[:], offs3)
        nc.sync.dma_start(lst4[:], offs4)
        nc.sync.dma_start(lst5[:], offs5)
        load_factor(nc.sync, fd, sd)
        nc.sync.dma_start(lst6[:], offs6)
        for slot, tile, words, scales in ((SLOT_WS, ws_w, ws_words, ws_scales), (SLOT_WB, wb_w, wb_words, wb_scales)):
            load_fp8_words(tile, words)
            for q in range(QUADS):
                load_rows(s2[:, slot * N : (slot + 1) * N], scales, q)

        for q in range(QUADS):
            nc.vector.tensor_copy(out=s1_raw[QUAD * q : QUAD * q + SCALE_ROWS, :].bitcast(I32), in_=stage[:, q, :])
        s1_view = s1_raw[:].rearrange("p (s m t) -> p t s m", s=2, t=PACK)
        s1_early = new_tile("s1_early", [P, EARLY_TILES, 2, P], U8)
        for t in range(EARLY_TILES):
            nc.vector.tensor_copy(out=s1_early[:, t], in_=s1_view[:, t])

        w_p = new_tile("w_p", [P, PACK, P], U16)
        w0_p = new_tile("w0_p", [P, PACK, P], U32)
        w_view = w_raw[:].rearrange("p (m t) -> p t m", t=PACK)
        w0_view = w0_raw[:].rearrange("p (m t) -> p m t", t=PACK)
        nc.scalar.copy(out=w_p[:, 0, :], in_=w_view[:, 0, :])
        nc.scalar.copy(out=w0_p[:, 0, :], in_=w0_view[:, :, 0])
        nc.scalar.copy(out=w_p[:, 1:PACK, :], in_=w_view[:, 1:PACK, :])
        nc.scalar.copy(out=w0_p[:, 1:PACK, :].rearrange("p t m -> p m t"), in_=w0_view[:, :, 1:PACK])

        j_half = J // HALVES
        j_cols = [slice(u * j_half, (u + 1) * j_half) for u in range(HALVES)]
        og_w = new_tile("og_w", [P, J], U16)
        og_s = new_tile("og_s", [P, J], U8)
        tg_w = tile_in("tg_w", "tg_w", [P, J], U32)
        tg_s = tile_in("tg_s", "tg_s", [P, J], U8)
        nc.vector.tensor_copy(out=tg_w[:], in_=xt_w[:].indirect(lst1[:]))
        nc.vector.tensor_copy(out=og_w[:], in_=xo_w[:].indirect(lst2[:]))
        nc.vector.tensor_copy(out=tg_s[:], in_=xt_s[:].indirect(lst1[:]))
        for u in range(HALVES):
            entries = lst2[:, u * j_half // PER_COLUMN : (u + 1) * j_half // PER_COLUMN]
            nc.vector.tensor_copy(out=og_s[:, j_cols[u]], in_=xo_s[:].indirect(entries))

        s1_late = tile_in("xo_s", "s1_late", [P, PACK - EARLY_TILES, 2, P], U8)
        for t in range(EARLY_TILES, PACK):
            nc.vector.tensor_copy(out=s1_late[:, t - EARLY_TILES], in_=s1_view[:, t])
        s1 = [s1_early[:, t] for t in range(EARLY_TILES)] + [s1_late[:, t] for t in range(PACK - EARLY_TILES)]

        def first_stage(t, acc, cols):
            nc.tensor.matmul_mx(
                out=acc[:], lhsT=w_p[:, t, :].bitcast(E2M1), lhsT_scale=s1[t][:, SLOT_W, :],
                rhs=tg_w[:, cols].bitcast(E4M3), rhs_scale=tg_s[:, cols], start=True, stop=False,
            )
            nc.tensor.matmul_mx(
                out=acc[:], lhsT=w0_p[:, t, :].bitcast(E5M2), lhsT_scale=s1[t][:, SLOT_W0, :],
                rhs=og_w[:, cols].bitcast(E2M1), rhs_scale=og_s[:, cols], start=False, stop=True,
            )

        rows_a = [new_tile(f"a{t}", [P, J], F32) for t in range(PACK)]
        for u in range(HALVES):
            acc = psum.tile([P, j_half], F32, name=f"acc0_{u}")
            first_stage(0, acc, j_cols[u])
            nc.scalar.copy(out=rows_a[0][:, j_cols[u]], in_=acc[:])
        for t in range(1, PACK):
            acc = psum.tile([P, J], F32, name=f"acc{t}")
            first_stage(t, acc, slice(0, J))
            nc.vector.tensor_copy(out=rows_a[t][:], in_=acc[:])

        x6_w = tile_in("tg_w", "x6_w", [P, O], U32)
        x6_s = tile_in("tg_s", "x6_s", [P, O], U8)
        nc.vector.tensor_copy(out=x6_w[:], in_=xt_w[:].indirect(lst6[:]))
        nc.vector.tensor_copy(out=x6_s[:], in_=xt_s[:].indirect(lst6[:]))
        sums = []
        for h in range(N // P):
            y = psum.tile([P, O], F32, name=f"y{h}")
            nc.tensor.matmul_mx(
                out=y[:], lhsT=ws_w[:, h * P : (h + 1) * P].bitcast(E5M2),
                lhsT_scale=s2[:, SLOT_WS * N + h * P : SLOT_WS * N + (h + 1) * P],
                rhs=x6_w[:].bitcast(E4M3), rhs_scale=x6_s[:], start=True, stop=False,
            )
            sums.append(y)

        def look_up(dst, t, entries, factor):
            nc.scalar.activation(out=dst[:], in_=rows_a[t][:].indirect(entries), func=ACT.Copy, scale=factor[:, t : t + 1])

        o_half = O // HALVES
        o_cols = [slice(u * o_half, (u + 1) * o_half) for u in range(HALVES)]
        totals = [new_tile(f"total{u}", [P, PACK, o_half], F32) for u in range(HALVES)]
        for t in range(PACK):
            ga = new_tile(f"ga{t}", [P, O], F32)
            gb = new_tile(f"gb{t}", [P, O], F32)
            part = new_tile(f"part{t}", [P, O], F32)
            look_up(ga, t, lst3[:], fa)
            look_up(gb, t, lst4[:], fb)
            nc.vector.tensor_tensor(out=part[:], in0=ga[:], in1=gb[:], op=ALU.add)
            if t < PACK - 1:
                gd = new_tile(f"gd{t}", [P, O], F32)
                look_up(gd, t, lst5[:], fd)
                for u in range(HALVES):
                    nc.vector.tensor_tensor(
                        out=totals[u][:, t, :], in0=part[:, o_cols[u]], in1=gd[:, o_cols[u]], op=ALU.add
                    )
            else:
                for u in range(HALVES):
                    gd_half = new_tile(f"gd{t}_{u}", [P, o_half], F32)
                    look_up(gd_half, t, lst5[:, u * o_half // PER_COLUMN : (u + 1) * o_half // PER_COLUMN], fd)
                    nc.vector.tensor_tensor(
                        out=totals[u][:, t, :], in0=part[:, o_cols[u]], in1=gd_half[:], op=ALU.add
                    )

        hq_w = new_tile("hq_w", [P, O], U32)
        hq_s = new_tile("hq_s", [P, O], U8)
        hids = [new_tile(f"hid{u}", [P, o_half, PACK], BF16) for u in range(HALVES)]
        for u in range(HALVES):
            nc.vector.tensor_scalar(
                out=hids[u][:], in0=totals[u][:].rearrange("p t o -> p o t"), scalar1=0.0, scalar2=None, op0=ALU.max
            )
        for u in range(HALVES):
            nc.vector.quantize_mx(
                out=hq_w[:, o_cols[u]].bitcast(E4M3), scales=hq_s[:, o_cols[u]],
                in_=hids[u][:].rearrange("p o t -> p (o t)"),
            )

        for h in range(N // P):
            nc.tensor.matmul_mx(
                out=sums[h][:], lhsT=wb_w[:, h * P : (h + 1) * P].bitcast(E5M2),
                lhsT_scale=s2[:, SLOT_WB * N + h * P : SLOT_WB * N + (h + 1) * P],
                rhs=hq_w[:].bitcast(E4M3), rhs_scale=hq_s[:], start=False, stop=True,
            )
        results = [new_tile(f"res{h}", [P, O], F32) for h in range(N // P)]
        for h in range(N // P):
            nc.vector.tensor_copy(out=results[h][:], in_=sums[h][:])
            nc.sync.dma_start(out=out[h * P : (h + 1) * P, :], in_=results[h][:])
